import numpy as np
import ml_dtypes


def mxq(x, axis, fmt="e4m3"):
    dtype, down = {"e4m3": (ml_dtypes.float8_e4m3fn, 7), "e5m2": (ml_dtypes.float8_e5m2, 14)}[fmt]
    v = np.moveaxis(np.asarray(x, np.float32).astype(ml_dtypes.bfloat16).astype(np.float64), axis, -1)
    blocks = v.reshape(v.shape[:-1] + (-1, 32))
    amax = np.abs(blocks).max(-1, keepdims=True)
    byte = np.maximum(np.where(amax > 0, np.frexp(amax)[1] - 1 + 127, 0) - down, 1)
    scale = np.exp2(byte - 127.0)
    codes = (blocks / scale).astype(np.float32).astype(dtype).astype(np.float64)
    return np.moveaxis((codes * scale).reshape(v.shape), -1, axis)


WIDE = False


def mx_kscale(k):
    if not WIDE:
        return np.ones(k)
    levels = np.array([10, -10, 5, -5, 0])
    if k % 512:
        return np.exp2(np.random.permutation(np.resize(levels, k // 32))).repeat(32)
    a = np.empty((k // 512, 16))
    for p in range(k // 512):
        a[p, :8] = np.random.permutation(np.resize(levels, 8))
        for g in range(8):
            far = levels[np.abs(levels - a[p, g]) >= 10]
            a[p, g + 8] = far[np.random.randint(len(far))]
    return np.exp2(a.ravel()).repeat(32)


def f64(x):
    return np.asarray(x).astype(np.float64)


def striped(idx):
    return np.tile(idx.reshape(-1, 16).T, (8, 1)).astype(np.uint16)


def unstriped(offs):
    return offs[:16].T.reshape(-1).astype(np.int64)


E2M1 = np.array([0.0, 0.5, 1.0, 1.5, 2.0, 3.0, 4.0, 6.0, -0.0, -0.5, -1.0, -1.5, -2.0, -3.0, -4.0, -6.0])


def pack_weight(w, fmt):
    k, n = w.shape
    w = f64(np.asarray(w, np.float32).astype(ml_dtypes.bfloat16)).reshape(k // 32, 32, n)
    amax = np.abs(w).max(1)
    if fmt == "e4m3":
        byte = np.frexp(amax)[1] - 1 + 127 - 7
    else:
        mant, ex = np.frexp(amax / 6.0)
        byte = np.where(mant > 0.5, ex, ex - 1) + 127
    byte = np.clip(np.where(amax > 0, byte, 1), 1, 254)
    scaled = (w * np.exp2(127.0 - byte)[:, None, :]).reshape(k, n).astype(np.float32)
    by_word = np.ascontiguousarray(scaled.reshape(k // 512, 128, 4, n).transpose(0, 1, 3, 2))
    if fmt == "e4m3":
        words = by_word.astype(ml_dtypes.float8_e4m3fn).view(np.uint8)
    else:
        c = by_word.astype(ml_dtypes.float4_e2m1fn).view(np.uint8) & 0xF
        words = (c[..., 0::2] | (c[..., 1::2] << 4)).reshape(k // 512, 128, 2 * n)
    return np.ascontiguousarray(words), np.ascontiguousarray(byte.astype(np.uint8).reshape(k // 512, 16, n))


def unpack_weight(words, scales, fmt):
    g, _, n = scales.shape
    words = np.ascontiguousarray(words).reshape(g, 128, n, -1)
    if fmt == "e4m3":
        vals = words.view(ml_dtypes.float8_e4m3fn).astype(np.float64)
    else:
        nib = np.empty((g, 128, n, 4), np.uint8)
        nib[..., 0::2] = words & 0xF
        nib[..., 1::2] = words >> 4
        vals = E2M1[nib]
    vals = vals * np.repeat(np.exp2(scales.astype(np.float64) - 127.0), 8, axis=1)[..., None]
    return vals.transpose(0, 1, 3, 2).reshape(g * 512, n)


def gelu(v):
    return 0.5 * v * (1.0 + np.tanh(np.sqrt(2.0 / np.pi) * (v + 0.044715 * v**3)))


def striped8(idx):
    return np.concatenate([v.reshape(-1, 16).T for v in idx]).astype(np.uint16)


def unstriped8(offs):
    return np.stack([offs[16 * g:16 * g + 16].T.reshape(-1) for g in range(8)]).astype(np.int64)


def runs(v, idx8):
    k = np.arange(v.shape[0])
    return v[k[:, None], idx8[k % 512 // 64]]


K, K2, H, T, S, T2 = 1024, 512, 1024, 2048, 1024, 2048

def setup_inputs():
    n = np.random.standard_normal
    s1 = mx_kscale(K)[:, None]
    s2 = mx_kscale(K2)[:, None]
    u = mx_kscale(H)[:, None]
    tab_words, tab_scales = pack_weight(n((K, T)) * s1, "e4m3")
    tab2_words, tab2_scales = pack_weight(n((K2, T)) * s2, "e4m3")
    w1_words, w1_scales = pack_weight(1.1 * n((K, H)) / np.sqrt(K) / s1, "e2m1")
    w2 = (0.42 * n((K2, H)) / np.sqrt(K2) / s2).astype(np.float32)
    gain = (np.random.uniform(0.5, 1.5, H) * u[:, 0]).astype(np.float32)
    w3 = (1.6 * n((H, H)) / np.sqrt(H) / u).astype(np.float32)
    phase = np.random.uniform(-0.6, 0.6, H).astype(np.float32)
    page1 = n((H, T2)).astype(np.float32)
    wgo = np.exp(0.3 * n((128, S))).astype(np.float32)
    offs = striped8(np.stack([np.random.permutation(T)[:S] for _ in range(8)]))
    offs2 = striped(np.random.permutation(T)[:S])
    offs3 = striped(np.random.permutation(T2)[:S])
    return {"tab_words": tab_words, "tab_scales": tab_scales, "tab2_words": tab2_words, "tab2_scales": tab2_scales,
            "offs": offs, "offs2": offs2, "offs3": offs3, "w1_words": w1_words, "w1_scales": w1_scales,
            "w2": w2, "gain": gain, "w3": w3, "phase": phase, "page1": page1, "wgo": wgo}

def reference(tab_words, tab_scales, tab2_words, tab2_scales, offs, offs2, offs3, w1_words, w1_scales,
              w2, gain, w3, phase, page1, wgo):
    v = runs(unpack_weight(tab_words, tab_scales, "e4m3"), unstriped8(offs))
    v2 = unpack_weight(tab2_words, tab2_scales, "e4m3")[:, unstriped(offs2)]
    w1 = unpack_weight(w1_words, w1_scales, "e2m1")
    stroke = w1.T @ v
    bell = mxq(f64(w2), 0, "e4m3").T @ v2
    h = np.tanh(stroke + bell) * f64(gain)[:, None]
    y = mxq(f64(w3), 0, "e4m3").T @ mxq(h, 0, "e4m3")
    y = y * np.cos(bell + f64(phase)[:, None])
    out = f64(page1).copy()
    out[:, unstriped(offs3)] = np.tile(f64(wgo), (H // 128, 1)) * y
    return out

@@ -1,0 +1,302 @@
+import math
+from contextlib import ExitStack
+
+import concourse.mybir as mybir
+
+K, K2, H, T, S, T2 = 1024, 512, 1024, 2048, 1024, 2048
+FLOPS = 2 * S * H * (K + K2 + H)
+
+F32 = mybir.dt.float32
+BF16 = mybir.dt.bfloat16
+I32 = mybir.dt.int32
+U32 = mybir.dt.uint32
+U16 = mybir.dt.uint16
+U8 = mybir.dt.uint8
+FP8X4 = mybir.dt.float8_e4m3fn_x4
+FP4X4 = mybir.dt.float4_e2m1fn_x4
+ALU = mybir.AluOpType
+ACT = mybir.ActivationFunctionType
+
+P = 128
+N = 512
+TWO_PI = 2.0 * math.pi
+ROOM = 8192
+
+
+def tile_list_carillon_strike_coach_kernel(
+    tc, tab_words, tab_scales, tab2_words, tab2_scales, offs, offs2, offs3,
+    w1_words, w1_scales, w2, gain, w3, phase, page1, wgo, out,
+):
+    nc = tc.nc
+    with ExitStack() as ctx:
+        keep = ctx.enter_context(tc.tile_pool(name="keep", bufs=1))
+        rooms = ctx.enter_context(tc.tile_pool(name="rooms", bufs=1))
+        work = ctx.enter_context(tc.tile_pool(name="work", bufs=2))
+        psum = ctx.enter_context(tc.psum_pool(name="psum", bufs=1))
+
+        def in_room(room, shape, dtype, name):
+            return rooms.tile(shape, dtype, name=name, offset=int(room * ROOM), align_bytes=64)
+
+        list1 = keep.tile([P, S // 16], U16, name="list1")
+        list2 = keep.tile([P, S // 16], U16, name="list2")
+        list3 = keep.tile([P, S // 16], U16, name="list3")
+        gain_t = keep.tile([P, 2, 4], F32, name="gain_t")
+        phase_t = keep.tile([P, 2, 4], F32, name="phase_t")
+
+        tab_sc = in_room(2, [P, T], U8, "tab_sc")
+        tab2_sc = in_room(3.875, [P, T], U8, "tab2_sc")
+        w1_sc_raw = in_room(7, [P, 2 * H], U8, "w1_sc_raw")
+        v_sc = [keep.tile([P, S], U8, name="v_sc%d" % a, align_bytes=64) for a in range(2)]
+        nc.vector.memset(tab_sc[:].bitcast(I32), 0)
+        nc.vector.memset(tab2_sc[:].bitcast(I32), 0)
+        nc.vector.memset(w1_sc_raw[:].bitcast(I32), 0)
+        for a in range(2):
+            nc.vector.memset(v_sc[a][:].bitcast(I32), 0)
+
+        def load_words(room, src, name):
+            tile = in_room(room, [P, T], I32, name)
+            nc.sync.dma_start(tile[:], src.rearrange("p t i -> p (t i)").bitcast(I32))
+            return tile
+
+        def load_weight(room, w, a, b, name):
+            tile = in_room(room, [P, 4, N], F32, name)
+            rows = w[N * a : N * (a + 1), N * b : N * (b + 1)]
+            nc.sync.dma_start(tile[:], rows.rearrange("(p j) c -> p j c", j=4))
+            return tile
+
+        def load_wgo(room, half):
+            tile = in_room(room, [P, 4 * N], F32, "wgo%d" % half)
+            rows = wgo[:, N * half : N * (half + 1)].rearrange("(p t) j -> p t j", t=4)
+            for d in range(4):
+                nc.sync.dma_start(tile[32 * d : 32 * (d + 1), :].rearrange("p (t j) -> p t j", t=4), rows)
+            return tile
+
+        page_rows = page1.rearrange("(b p t) c -> b t p c", b=2, t=4)
+        out_rows = out.rearrange("(b p t) c -> b t p c", b=2, t=4)
+        pages = {}
+
+        def load_page(room, m):
+            pages[m] = in_room(room, [P, T2], F32, "page%d" % m)
+            nc.sync.dma_start(pages[m][:], page_rows[m // 4, m % 4])
+
+        nc.sync.dma_start(list1[:], offs)
+        nc.sync.dma_start(list2[:], offs2)
+        nc.sync.dma_start(list3[:], offs3)
+        nc.sync.dma_start(phase_t[:], phase.rearrange("(b p t) -> p b t", b=2, t=4))
+        nc.sync.dma_start(gain_t[:], gain.rearrange("(b p t) -> p b t", b=2, t=4))
+        tab2_w = load_words(0.5, tab2_words[0], "tab2_w")
+        w2_raw = load_weight(8, w2, 0, 0, "w2_raw0")
+        for a in range(2):
+            nc.scalar.dma_start(tab_sc[a:P:8, :].bitcast(I32), tab_scales[a].bitcast(I32))
+        for r in range(4):
+            nc.scalar.dma_start(tab2_sc[r:P:32, :].bitcast(I32), tab2_scales[0, r:16:4, :].bitcast(I32))
+        for r in range(4):
+            nc.scalar.dma_start(
+                w1_sc_raw[r:P:32, :].bitcast(I32).rearrange("p (a c) -> p a c", a=2),
+                w1_scales[:, r:16:4, :].rearrange("a q c -> q a c").bitcast(I32),
+            )
+
+        def quantise(grouped, name):
+            codes = keep.tile([P, N], U32, name=name + "_codes", align_bytes=64)
+            scales = keep.tile([P, N], U8, name=name + "_scales", align_bytes=64)
+            nc.vector.quantize_mx(out=codes[:].bitcast(FP8X4), scales=scales[:], in_=grouped[:])
+            return codes, scales
+
+        def bf16_tile(name):
+            return work.tile([P, 4 * N], BF16, name=name, tag="bf", bufs=4, align_bytes=64)
+
+        def quantise_weight(raw, name):
+            grouped = bf16_tile("grouped")
+            nc.scalar.copy(
+                grouped[:].rearrange("p (t m j) -> p m j t", t=4, j=4),
+                raw[:].rearrange("p j (m t) -> p m j t", t=4),
+            )
+            return quantise(grouped, name)
+
+        picked_sc = keep.tile([P, S], U8, name="picked_sc", align_bytes=64)
+        nc.vector.tensor_copy(picked_sc[:], tab_sc[:].indirect(list1[:]))
+        for a in range(2):
+            for r in range(4):
+                nc.sync.dma_start(v_sc[a][r:P:32, :].bitcast(I32), picked_sc[8 * r + a : P : 32, :].bitcast(I32))
+        v2_w = keep.tile([P, S], U32, name="v2_w", align_bytes=64)
+        nc.vector.tensor_copy(v2_w[:], tab2_w[:].bitcast(U32).indirect(list2[:]))
+        tab_w = [load_words(a, tab_words[a], "tab_w%d" % a) for a in range(2)]
+        w1_raw = in_room(2, [P, 2, 2 * H // 4], I32, "w1_raw")
+        nc.sync.dma_start(w1_raw[:], w1_words.rearrange("a p c -> p a c").bitcast(I32))
+        v2_sc = keep.tile([P, S], U8, name="v2_sc", align_bytes=64)
+        nc.vector.tensor_copy(v2_sc[:], tab2_sc[:].indirect(list2[:]))
+        w2_q = [quantise_weight(w2_raw, "w2_0")]
+        w2_raw = load_weight(8, w2, 0, 1, "w2_raw1")
+        w3_raw = {(a, 0): load_weight(3 + a, w3, a, 0, "w3_raw%d0" % a) for a in range(2)}
+
+        v_w = in_room(9, [P, 2 * S], U32, "v_w")
+
+        def gather_words(a, half):
+            first = S * a + N * half
+            cols = slice(half * N // 16, (half + 1) * N // 16)
+            nc.vector.tensor_copy(v_w[:, first : first + N], tab_w[a][:].bitcast(U32).indirect(list1[:, cols]))
+
+        w1_w = keep.tile([P, 2 * 2 * H], U8, name="w1_w", align_bytes=64)
+        w1_sc = keep.tile([P, 2 * H], U8, name="w1_sc", align_bytes=64)
+        gather_words(0, 0)
+        gather_words(1, 0)
+        nc.vector.tensor_copy(
+            w1_w[:].bitcast(U16).rearrange("p (g t m) -> p g t m", g=4, t=4),
+            w1_raw[:].rearrange("p a c -> p (a c)").bitcast(U16).rearrange("p (g m t) -> p g t m", g=4, t=4),
+        )
+        nc.vector.tensor_copy(
+            w1_sc[:].rearrange("p (g t m) -> p g t m", g=4, t=4),
+            w1_sc_raw[:].rearrange("p (g m t) -> p g t m", g=4, t=4),
+        )
+        w2_q.append(quantise_weight(w2_raw, "w2_1"))
+        gather_words(0, 1)
+        gather_words(1, 1)
+        wgo_t = [load_wgo(0, 0)]
+        load_page(2, 0)
+        w3_raw[0, 1] = load_weight(7, w3, 0, 1, "w3_raw01")
+        w3_raw[1, 1] = load_weight(8, w3, 1, 1, "w3_raw11")
+        load_page(1, 1)
+
+        def bank(tag, bufs):
+            return psum.tile([P, N], F32, name=tag, tag=tag, bufs=bufs)
+
+        def bell_pass(acc, m, half, start, stop):
+            codes, scales = w2_q[m // 4]
+            cols = slice(P * (m % 4), P * (m % 4 + 1))
+            picks = slice(N * half, N * (half + 1))
+            nc.tensor.matmul_mx(
+                out=acc[:], lhsT=codes[:, cols].bitcast(FP8X4), lhsT_scale=scales[:, cols],
+                rhs=v2_w[:, picks].bitcast(FP8X4), rhs_scale=v2_sc[:, picks], start=start, stop=stop,
+            )
+
+        def stroke_passes(acc, m, half, start):
+            for a in range(2):
+                first = H * a + P * m
+                picks = S * a + N * half
+                nc.tensor.matmul_mx(
+                    out=acc[:], lhsT=w1_w[:, 2 * first : 2 * (first + P)].bitcast(FP4X4),
+                    lhsT_scale=w1_sc[:, first : first + P],
+                    rhs=v_w[:, picks : picks + N].bitcast(FP8X4), rhs_scale=v_sc[a][:, N * half : N * (half + 1)],
+                    start=(start and a == 0), stop=(a == 1),
+                )
+
+        def f32_tile(tag, bufs, dtype=F32):
+            return work.tile([P, N], dtype, name=tag, tag=tag, bufs=bufs)
+
+        def column(vector, m):
+            return vector[:, m // 4, m % 4 : m % 4 + 1]
+
+        angle, rest, factor = {}, {}, {}
+
+        def reduce_angle(m, half):
+            size = f32_tile("size", 2)
+            if half == 0:
+                bell = bank("bell", 2)
+                bell_pass(bell, m, half, True, True)
+                nc.scalar.activation(size[:], bell[:], ACT.Abs, bias=column(phase_t, m))
+            else:
+                nc.scalar.activation(size[:], angle[m][:], ACT.Abs)
+            turns = f32_tile("turns", 2, I32)
+            nc.scalar.activation(turns[:].bitcast(U32), size[:], ACT.Copy, bias=0.25, scale=1.0 / TWO_PI)
+            rest[m, half] = f32_tile("rest", 3)
+            nc.vector.scalar_tensor_tensor(rest[m, half][:], turns[:], -TWO_PI, size[:], ALU.mult, ALU.add)
+
+        def take_cosine(m, half):
+            cosine = f32_tile("cosine", 3)
+            nc.scalar.activation(cosine[:], rest[m, half][:], ACT.Sin, bias=math.pi / 2)
+            factor[m, half] = cosine
+
+        w3_q, h_q = {}, {}
+
+        def first_features(b):
+            bent = in_room(5 + b, [P, 4, N], F32, "bent4_%d" % b)
+            for t in range(4):
+                m = 4 * b + t
+                acc = bank("sum", 3)
+                bell_pass(acc, m, 0, True, False)
+                stroke_passes(acc, m, 0, False)
+                nc.scalar.activation(bent[:, t, :], acc[:], ACT.Tanh)
+            grouped = bf16_tile("grouped")
+            nc.vector.tensor_tensor(
+                grouped[:].rearrange("p (c i t) -> p c t i", i=4, t=4),
+                bent[:].rearrange("p t (c i) -> p c t i", i=4),
+                gain_t[:, b : b + 1, :].unsqueeze(3).to_broadcast([P, N // 4, 4, 4]),
+                ALU.mult,
+            )
+            h_q[b, 0] = quantise(grouped, "h%d0" % b)
+            load_page(5 + b, 4 + b)
+
+        planes = {}
+
+        def second_features(m):
+            b, t = divmod(m, 4)
+            if t == 0:
+                planes[b] = bf16_tile("planes")
+            bell = bank("bell", 2)
+            bell_pass(bell, m, 1, True, True)
+            angle[m] = f32_tile("angle", 8)
+            nc.scalar.activation(angle[m][:], bell[:], ACT.Identity, bias=column(phase_t, m))
+            acc = bank("sum", 3)
+            stroke_passes(acc, m, 1, True)
+            joint = f32_tile("joint", 3)
+            nc.vector.scalar_tensor_tensor(joint[:], acc[:], column(phase_t, m), angle[m][:], ALU.subtract, ALU.add)
+            bent = f32_tile("bent", 2)
+            nc.scalar.activation(bent[:], joint[:], ACT.Tanh)
+            nc.scalar.activation(planes[b][:, N * t : N * (t + 1)], bent[:], ACT.Copy, scale=column(gain_t, m))
+            if t == 3:
+                grouped = bf16_tile("grouped")
+                nc.scalar.copy(
+                    grouped[:].rearrange("p (c i t) -> p c t i", i=4, t=4),
+                    planes[b][:].rearrange("p (t c i) -> p c t i", i=4, t=4),
+                )
+                h_q[b, 1] = quantise(grouped, "h%d1" % b)
+
+        def place(m, half):
+            b, t = divmod(m, 4)
+            acc = bank("y", 3)
+            cols = slice(P * t, P * (t + 1))
+            for a in range(2):
+                nc.tensor.matmul_mx(
+                    out=acc[:], lhsT=w3_q[a, b][0][:, cols].bitcast(FP8X4), lhsT_scale=w3_q[a, b][1][:, cols],
+                    rhs=h_q[a, half][0][:].bitcast(FP8X4), rhs_scale=h_q[a, half][1][:],
+                    start=(a == 0), stop=(a == 1),
+                )
+            window = pages[m][:].indirect(list3[:, half * N // 16 : (half + 1) * N // 16])
+            z = f32_tile("z", 3)
+            nc.vector.tensor_tensor(z[:], acc[:], factor[m, half][:], ALU.mult)
+            if (m, half) in ((0, 0), (0, 1)):
+                clock = keep.tile([P, 1], F32, name="clock%d%d" % (m, half))
+                nc.gpsimd.tensor_copy(clock[:], z[:, 0:1])
+            nc.vector.tensor_tensor(window, z[:], wgo_t[half][:, N * t : N * (t + 1)], ALU.mult)
+            if half == 1:
+                nc.sync.dma_start(out_rows[b, t], pages[m][:])
+
+        for b in range(2):
+            first_features(b)
+        for a in range(2):
+            w3_q[a, 0] = quantise_weight(w3_raw[a, 0], "w3_%d0" % a)
+            load_page(3 + a, 2 + a)
+        reduce_angle(0, 0)
+        take_cosine(0, 0)
+        for m in range(8):
+            if m < 7:
+                reduce_angle(m + 1, 0)
+            place(m, 0)
+            if m in (0, 1):
+                a = (0, 1).index(m)
+                w3_q[a, 1] = quantise_weight(w3_raw[a, 1], "w3_%d1" % a)
+                load_page(7 + a, 6 + a)
+            for j in ((0,), (1,), (2, 3), (4,), (5, 6), (7,), (), ())[m]:
+                second_features(j)
+            if m < 7:
+                take_cosine(m + 1, 0)
+            if m == 6:
+                wgo_t.append(load_wgo(9, 1))
+                reduce_angle(0, 1)
+                take_cosine(0, 1)
+        for m in range(8):
+            if m < 7:
+                reduce_angle(m + 1, 1)
+            place(m, 1)
+            if m < 7:
+                take_cosine(m + 1, 1)

@@ -43,15 +43,19 @@ def tile_list_carillon_strike_coach_kernel(
         gain_t = keep.tile([P, 2, 4], F32, name="gain_t")
         phase_t = keep.tile([P, 2, 4], F32, name="phase_t")
 
-        tab_sc = in_room(2, [P, T], U8, "tab_sc")
-        tab2_sc = in_room(3.875, [P, T], U8, "tab2_sc")
+        tab_sc = in_room(10, [P, T], U8, "tab_sc")
+        tab2_sc = in_room(4, [P, T], U8, "tab2_sc")
         w1_sc_raw = in_room(7, [P, 2 * H], U8, "w1_sc_raw")
         v_sc = [keep.tile([P, S], U8, name="v_sc%d" % a, align_bytes=64) for a in range(2)]
-        nc.vector.memset(tab_sc[:].bitcast(I32), 0)
+        nc.gpsimd.memset(tab_sc[:].bitcast(I32), 0)
         nc.vector.memset(tab2_sc[:].bitcast(I32), 0)
         nc.vector.memset(w1_sc_raw[:].bitcast(I32), 0)
         for a in range(2):
             nc.vector.memset(v_sc[a][:].bitcast(I32), 0)
+
+        warm = keep.tile([P, 2], F32, name="warm")
+        nc.vector.memset(warm[:, 0:1], 0.0)
+        nc.scalar.activation(warm[:, 1:2], warm[:, 0:1], ACT.Silu)
 
         def load_words(room, src, name):
             tile = in_room(room, [P, T], I32, name)
@@ -81,20 +85,23 @@ def tile_list_carillon_strike_coach_kernel(
 
         nc.sync.dma_start(list1[:], offs)
         nc.sync.dma_start(list2[:], offs2)
-        nc.sync.dma_start(list3[:], offs3)
-        nc.sync.dma_start(phase_t[:], phase.rearrange("(b p t) -> p b t", b=2, t=4))
-        nc.sync.dma_start(gain_t[:], gain.rearrange("(b p t) -> p b t", b=2, t=4))
-        tab2_w = load_words(0.5, tab2_words[0], "tab2_w")
-        w2_raw = load_weight(8, w2, 0, 0, "w2_raw0")
         for a in range(2):
-            nc.scalar.dma_start(tab_sc[a:P:8, :].bitcast(I32), tab_scales[a].bitcast(I32))
+            nc.sync.dma_start(tab_sc[a:P:8, :].bitcast(I32), tab_scales[a].bitcast(I32))
+        tab2_w = load_words(3, tab2_words[0], "tab2_w")
         for r in range(4):
-            nc.scalar.dma_start(tab2_sc[r:P:32, :].bitcast(I32), tab2_scales[0, r:16:4, :].bitcast(I32))
+            nc.sync.dma_start(tab2_sc[r:P:32, :].bitcast(I32), tab2_scales[0, r:16:4, :].bitcast(I32))
+        w2_raw = load_weight(8, w2, 0, 0, "w2_raw0")
+        tab_w = [load_words(a, tab_words[a], "tab_w%d" % a) for a in range(2)]
+        w1_raw = in_room(2, [P, 2, 2 * H // 4], I32, "w1_raw")
+        nc.sync.dma_start(w1_raw[:], w1_words.rearrange("a p c -> p a c").bitcast(I32))
         for r in range(4):
-            nc.scalar.dma_start(
+            nc.sync.dma_start(
                 w1_sc_raw[r:P:32, :].bitcast(I32).rearrange("p (a c) -> p a c", a=2),
                 w1_scales[:, r:16:4, :].rearrange("a q c -> q a c").bitcast(I32),
             )
+        nc.gpsimd.dma_start(phase_t[:], phase.rearrange("(b p t) -> p b t", b=2, t=4))
+        nc.gpsimd.dma_start(gain_t[:], gain.rearrange("(b p t) -> p b t", b=2, t=4))
+        nc.sync.dma_start(list3[:], offs3)
 
         def quantise(grouped, name):
             codes = keep.tile([P, N], U32, name=name + "_codes", align_bytes=64)
@@ -105,8 +112,8 @@ def tile_list_carillon_strike_coach_kernel(
         def bf16_tile(name):
             return work.tile([P, 4 * N], BF16, name=name, tag="bf", bufs=4, align_bytes=64)
 
-        def quantise_weight(raw, name):
-            grouped = bf16_tile("grouped")
+        def quantise_weight(raw, name, room=None):
+            grouped = bf16_tile("grouped") if room is None else in_room(room, [P, 4 * N], BF16, "grouped_" + name)
             nc.scalar.copy(
                 grouped[:].rearrange("p (t m j) -> p m j t", t=4, j=4),
                 raw[:].rearrange("p j (m t) -> p m j t", t=4),
@@ -120,30 +127,27 @@ def tile_list_carillon_strike_coach_kernel(
                 nc.sync.dma_start(v_sc[a][r:P:32, :].bitcast(I32), picked_sc[8 * r + a : P : 32, :].bitcast(I32))
         v2_w = keep.tile([P, S], U32, name="v2_w", align_bytes=64)
         nc.vector.tensor_copy(v2_w[:], tab2_w[:].bitcast(U32).indirect(list2[:]))
-        tab_w = [load_words(a, tab_words[a], "tab_w%d" % a) for a in range(2)]
-        w1_raw = in_room(2, [P, 2, 2 * H // 4], I32, "w1_raw")
-        nc.sync.dma_start(w1_raw[:], w1_words.rearrange("a p c -> p a c").bitcast(I32))
         v2_sc = keep.tile([P, S], U8, name="v2_sc", align_bytes=64)
         nc.vector.tensor_copy(v2_sc[:], tab2_sc[:].indirect(list2[:]))
         w2_q = [quantise_weight(w2_raw, "w2_0")]
         w2_raw = load_weight(8, w2, 0, 1, "w2_raw1")
         w3_raw = {(a, 0): load_weight(3 + a, w3, a, 0, "w3_raw%d0" % a) for a in range(2)}
 
-        v_w = in_room(9, [P, 2 * S], U32, "v_w")
+        v_w = keep.tile([P, 2 * S], U32, name="v_w", align_bytes=64)
 
         def gather_words(a, half):
             first = S * a + N * half
             cols = slice(half * N // 16, (half + 1) * N // 16)
             nc.vector.tensor_copy(v_w[:, first : first + N], tab_w[a][:].bitcast(U32).indirect(list1[:, cols]))
 
-        w1_w = keep.tile([P, 2 * 2 * H], U8, name="w1_w", align_bytes=64)
+        w1_w = in_room(10, [P, 2 * 2 * H], U8, "w1_w")
         w1_sc = keep.tile([P, 2 * H], U8, name="w1_sc", align_bytes=64)
-        gather_words(0, 0)
-        gather_words(1, 0)
         nc.vector.tensor_copy(
             w1_w[:].bitcast(U16).rearrange("p (g t m) -> p g t m", g=4, t=4),
             w1_raw[:].rearrange("p a c -> p (a c)").bitcast(U16).rearrange("p (g m t) -> p g t m", g=4, t=4),
         )
+        gather_words(0, 0)
+        gather_words(1, 0)
         nc.vector.tensor_copy(
             w1_sc[:].rearrange("p (g t m) -> p g t m", g=4, t=4),
             w1_sc_raw[:].rearrange("p (g m t) -> p g t m", g=4, t=4),
@@ -188,23 +192,23 @@ def tile_list_carillon_strike_coach_kernel(
 
         angle, rest, factor = {}, {}, {}
 
+        def take_angle(m, half):
+            bell = bank("bell", 2)
+            bell_pass(bell, m, half, True, True)
+            angle[m, half] = f32_tile("angle", 16)
+            nc.scalar.activation(angle[m, half][:], bell[:], ACT.Identity, bias=column(phase_t, m))
+
         def reduce_angle(m, half):
-            size = f32_tile("size", 2)
-            if half == 0:
-                bell = bank("bell", 2)
-                bell_pass(bell, m, half, True, True)
-                nc.scalar.activation(size[:], bell[:], ACT.Abs, bias=column(phase_t, m))
-            else:
-                nc.scalar.activation(size[:], angle[m][:], ACT.Abs)
-            turns = f32_tile("turns", 2, I32)
-            nc.scalar.activation(turns[:].bitcast(U32), size[:], ACT.Copy, bias=0.25, scale=1.0 / TWO_PI)
+            turns = f32_tile("turns", 3, I32)
+            nc.gpsimd.tensor_scalar(turns[:], angle[m, half][:], 1.0 / TWO_PI, 0.25, ALU.mult, ALU.add)
             rest[m, half] = f32_tile("rest", 3)
-            nc.vector.scalar_tensor_tensor(rest[m, half][:], turns[:], -TWO_PI, size[:], ALU.mult, ALU.add)
+            nc.vector.scalar_tensor_tensor(rest[m, half][:], turns[:], -TWO_PI, angle[m, half][:], ALU.mult, ALU.add)
 
         def take_cosine(m, half):
-            cosine = f32_tile("cosine", 3)
+            cosine = f32_tile("cosine", 2)
             nc.scalar.activation(cosine[:], rest[m, half][:], ACT.Sin, bias=math.pi / 2)
-            factor[m, half] = cosine
+            factor[m, half] = f32_tile("factor", 4)
+            nc.gpsimd.tensor_tensor(factor[m, half][:], cosine[:], wgo_t[half][:, N * (m % 4) : N * (m % 4 + 1)], ALU.mult)
 
         w3_q, h_q = {}, {}
 
@@ -232,14 +236,11 @@ def tile_list_carillon_strike_coach_kernel(
             b, t = divmod(m, 4)
             if t == 0:
                 planes[b] = bf16_tile("planes")
-            bell = bank("bell", 2)
-            bell_pass(bell, m, 1, True, True)
-            angle[m] = f32_tile("angle", 8)
-            nc.scalar.activation(angle[m][:], bell[:], ACT.Identity, bias=column(phase_t, m))
+            take_angle(m, 1)
             acc = bank("sum", 3)
             stroke_passes(acc, m, 1, True)
             joint = f32_tile("joint", 3)
-            nc.vector.scalar_tensor_tensor(joint[:], acc[:], column(phase_t, m), angle[m][:], ALU.subtract, ALU.add)
+            nc.vector.scalar_tensor_tensor(joint[:], acc[:], column(phase_t, m), angle[m, 1][:], ALU.subtract, ALU.add)
             bent = f32_tile("bent", 2)
             nc.scalar.activation(bent[:], joint[:], ACT.Tanh)
             nc.scalar.activation(planes[b][:, N * t : N * (t + 1)], bent[:], ACT.Copy, scale=column(gain_t, m))
@@ -263,11 +264,10 @@ def tile_list_carillon_strike_coach_kernel(
                 )
             window = pages[m][:].indirect(list3[:, half * N // 16 : (half + 1) * N // 16])
             z = f32_tile("z", 3)
-            nc.vector.tensor_tensor(z[:], acc[:], factor[m, half][:], ALU.mult)
-            if (m, half) in ((0, 0), (0, 1)):
-                clock = keep.tile([P, 1], F32, name="clock%d%d" % (m, half))
-                nc.gpsimd.tensor_copy(clock[:], z[:, 0:1])
-            nc.vector.tensor_tensor(window, z[:], wgo_t[half][:, N * t : N * (t + 1)], ALU.mult)
+            y = f32_tile("y_sb", 2)
+            nc.scalar.copy(y[:], acc[:])
+            nc.gpsimd.tensor_tensor(z[:], y[:], factor[m, half][:], ALU.mult)
+            nc.vector.tensor_copy(window, z[:])
             if half == 1:
                 nc.sync.dma_start(out_rows[b, t], pages[m][:])
 
@@ -276,27 +276,23 @@ def tile_list_carillon_strike_coach_kernel(
         for a in range(2):
             w3_q[a, 0] = quantise_weight(w3_raw[a, 0], "w3_%d0" % a)
             load_page(3 + a, 2 + a)
-        reduce_angle(0, 0)
-        take_cosine(0, 0)
         for m in range(8):
-            if m < 7:
-                reduce_angle(m + 1, 0)
-            place(m, 0)
-            if m in (0, 1):
-                a = (0, 1).index(m)
-                w3_q[a, 1] = quantise_weight(w3_raw[a, 1], "w3_%d1" % a)
+            take_angle(m, 0)
+        for u in range(3):
+            reduce_angle(u, 0)
+        for u in range(2):
+            take_cosine(u, 0)
+        for u in range(16):
+            if u + 3 < 16:
+                reduce_angle((u + 3) % 8, (u + 3) // 8)
+            if u + 2 < 16:
+                take_cosine((u + 2) % 8, (u + 2) // 8)
+            place(u % 8, u // 8)
+            if u in (0, 1):
+                a = (0, 1).index(u)
+                w3_q[a, 1] = quantise_weight(w3_raw[a, 1], "w3_%d1" % a, 9 if a == 1 else None)
                 load_page(7 + a, 6 + a)
-            for j in ((0,), (1,), (2, 3), (4,), (5, 6), (7,), (), ())[m]:
+                if a == 1:
+                    wgo_t.append(load_wgo(9, 1))
+            for j in {0: (0,), 1: (1,), 2: (2, 3), 3: (4,), 4: (5, 6), 5: (7,)}.get(u, ()):
                 second_features(j)
-            if m < 7:
-                take_cosine(m + 1, 0)
-            if m == 6:
-                wgo_t.append(load_wgo(9, 1))
-                reduce_angle(0, 1)
-                take_cosine(0, 1)
-        for m in range(8):
-            if m < 7:
-                reduce_angle(m + 1, 1)
-            place(m, 1)
-            if m < 7:
-                take_cosine(m + 1, 1)

@@ -19,8 +19,26 @@ ACT = mybir.ActivationFunctionType
 
 P = 128
 N = 512
+TILES = H // P
 TWO_PI = 2.0 * math.pi
-ROOM = 8192
+KIB = 1024
+
+AT_TAB0 = 0
+AT_TAB1 = 8
+AT_W1 = 16
+AT_TAB2 = 24
+AT_W2_FIRST = 32
+AT_BENT = (40, 48)
+AT_W3_LAST = 56
+AT_W2_SECOND = 64
+AT_W3_NEXT = 72
+AT_TAB_SCALES1 = 71
+AT_SECOND_PICKS = 80
+AT_W1_SCALES = 83.5
+
+SECOND_FEATURES_AFTER = {0: (0,), 1: (1,), 2: (2, 3), 3: (4,), 4: (5, 6), 5: (7,)}
+EARLY_ANGLES = 4
+ANGLE_LEAD = 2
 
 
 def tile_list_carillon_strike_coach_kernel(
@@ -30,12 +48,24 @@ def tile_list_carillon_strike_coach_kernel(
     nc = tc.nc
     with ExitStack() as ctx:
         keep = ctx.enter_context(tc.tile_pool(name="keep", bufs=1))
-        rooms = ctx.enter_context(tc.tile_pool(name="rooms", bufs=1))
+        shared = ctx.enter_context(tc.tile_pool(name="shared", bufs=1))
         work = ctx.enter_context(tc.tile_pool(name="work", bufs=2))
         psum = ctx.enter_context(tc.psum_pool(name="psum", bufs=1))
 
-        def in_room(room, shape, dtype, name):
-            return rooms.tile(shape, dtype, name=name, offset=int(room * ROOM), align_bytes=64)
+        def placed(start, shape, dtype, name):
+            return shared.tile(shape, dtype, name=name, offset=int(start * KIB), align_bytes=64)
+
+        def kept(shape, dtype, name):
+            return keep.tile(shape, dtype, name=name, align_bytes=64)
+
+        def bf16_tile(name):
+            return work.tile([P, 4 * N], BF16, name=name, tag="bf16", bufs=4, align_bytes=64)
+
+        def half_tile(tag, bufs, dtype=F32):
+            return work.tile([P, N], dtype, name=tag, tag=tag, bufs=bufs)
+
+        def bank(tag, bufs):
+            return psum.tile([P, N], F32, name=tag, tag=tag, bufs=bufs)
 
         list1 = keep.tile([P, S // 16], U16, name="list1")
         list2 = keep.tile([P, S // 16], U16, name="list2")
@@ -43,33 +73,32 @@ def tile_list_carillon_strike_coach_kernel(
         gain_t = keep.tile([P, 2, 4], F32, name="gain_t")
         phase_t = keep.tile([P, 2, 4], F32, name="phase_t")
 
-        tab_sc = in_room(10, [P, T], U8, "tab_sc")
-        tab2_sc = in_room(4, [P, T], U8, "tab2_sc")
-        w1_sc_raw = in_room(7, [P, 2 * H], U8, "w1_sc_raw")
-        v_sc = [keep.tile([P, S], U8, name="v_sc%d" % a, align_bytes=64) for a in range(2)]
-        nc.gpsimd.memset(tab_sc[:].bitcast(I32), 0)
-        nc.vector.memset(tab2_sc[:].bitcast(I32), 0)
-        nc.vector.memset(w1_sc_raw[:].bitcast(I32), 0)
-        for a in range(2):
-            nc.vector.memset(v_sc[a][:].bitcast(I32), 0)
+        tab_sc = [kept([P, T], U8, "tab_sc0"), placed(AT_TAB_SCALES1, [P, T], U8, "tab_sc1")]
+        tab2_sc = kept([P, T], U8, "tab2_sc")
+        w1_sc_raw = placed(AT_W1_SCALES, [P, 2 * H], U8, "w1_sc_raw")
+        v_sc = kept([P, 2 * S], U8, "v_sc")
+        nc.gpsimd.memset(tab_sc[0][:].bitcast(I32), 0)
+        nc.gpsimd.memset(tab2_sc[:].bitcast(I32), 0)
+        for tile in (tab_sc[1], w1_sc_raw, v_sc):
+            nc.vector.memset(tile[:].bitcast(I32), 0)
 
         warm = keep.tile([P, 2], F32, name="warm")
         nc.vector.memset(warm[:, 0:1], 0.0)
         nc.scalar.activation(warm[:, 1:2], warm[:, 0:1], ACT.Silu)
 
-        def load_words(room, src, name):
-            tile = in_room(room, [P, T], I32, name)
-            nc.sync.dma_start(tile[:], src.rearrange("p t i -> p (t i)").bitcast(I32))
+        def load_words(start, words, name):
+            tile = placed(start, [P, T], I32, name)
+            nc.sync.dma_start(tile[:], words.rearrange("p t i -> p (t i)").bitcast(I32))
             return tile
 
-        def load_weight(room, w, a, b, name):
-            tile = in_room(room, [P, 4, N], F32, name)
+        def load_weight(start, w, a, b, name):
+            tile = placed(start, [P, 4, N], F32, name)
             rows = w[N * a : N * (a + 1), N * b : N * (b + 1)]
             nc.sync.dma_start(tile[:], rows.rearrange("(p j) c -> p j c", j=4))
             return tile
 
-        def load_wgo(room, half):
-            tile = in_room(room, [P, 4 * N], F32, "wgo%d" % half)
+        def load_wgo(start, half):
+            tile = placed(start, [P, 4 * N], F32, "wgo%d" % half)
             rows = wgo[:, N * half : N * (half + 1)].rearrange("(p t) j -> p t j", t=4)
             for d in range(4):
                 nc.sync.dma_start(tile[32 * d : 32 * (d + 1), :].rearrange("p (t j) -> p t j", t=4), rows)
@@ -79,98 +108,106 @@ def tile_list_carillon_strike_coach_kernel(
         out_rows = out.rearrange("(b p t) c -> b t p c", b=2, t=4)
         pages = {}
 
-        def load_page(room, m):
-            pages[m] = in_room(room, [P, T2], F32, "page%d" % m)
+        def load_page(start, m):
+            pages[m] = placed(start, [P, T2], F32, "page%d" % m)
             nc.sync.dma_start(pages[m][:], page_rows[m // 4, m % 4])
 
         nc.sync.dma_start(list1[:], offs)
         nc.sync.dma_start(list2[:], offs2)
         for a in range(2):
-            nc.sync.dma_start(tab_sc[a:P:8, :].bitcast(I32), tab_scales[a].bitcast(I32))
-        tab2_w = load_words(3, tab2_words[0], "tab2_w")
-        for r in range(4):
-            nc.sync.dma_start(tab2_sc[r:P:32, :].bitcast(I32), tab2_scales[0, r:16:4, :].bitcast(I32))
-        w2_raw = load_weight(8, w2, 0, 0, "w2_raw0")
-        tab_w = [load_words(a, tab_words[a], "tab_w%d" % a) for a in range(2)]
-        w1_raw = in_room(2, [P, 2, 2 * H // 4], I32, "w1_raw")
-        nc.sync.dma_start(w1_raw[:], w1_words.rearrange("a p c -> p a c").bitcast(I32))
-        for r in range(4):
+            nc.sync.dma_start(tab_sc[a][0:P:8, :].bitcast(I32), tab_scales[a].bitcast(I32))
+        w2_raw = [load_weight(AT_W2_FIRST, w2, 0, 0, "w2_raw0")]
+        for d in range(4):
             nc.sync.dma_start(
-                w1_sc_raw[r:P:32, :].bitcast(I32).rearrange("p (a c) -> p a c", a=2),
-                w1_scales[:, r:16:4, :].rearrange("a q c -> q a c").bitcast(I32),
+                tab2_sc[32 * d : 32 * d + 4, :].bitcast(I32), tab2_scales[0, 4 * d : 4 * d + 4, :].bitcast(I32)
             )
-        nc.gpsimd.dma_start(phase_t[:], phase.rearrange("(b p t) -> p b t", b=2, t=4))
-        nc.gpsimd.dma_start(gain_t[:], gain.rearrange("(b p t) -> p b t", b=2, t=4))
+        tab2_w = load_words(AT_TAB2, tab2_words[0], "tab2_w")
+        nc.sync.dma_start(phase_t[:], phase.rearrange("(b p t) -> p b t", b=2, t=4))
+        tab_w = [load_words(AT_TAB0, tab_words[0], "tab_w0")]
+        for d in range(4):
+            nc.sync.dma_start(
+                w1_sc_raw[32 * d : 32 * d + 4, :].bitcast(I32).rearrange("p (a c) -> p a c", a=2),
+                w1_scales[:, 4 * d : 4 * d + 4, :].rearrange("a q c -> q a c").bitcast(I32),
+            )
+        w1_raw = placed(AT_W1, [P, 2, 2 * H // 4], I32, "w1_raw")
+        nc.sync.dma_start(w1_raw[:], w1_words.rearrange("a p c -> p a c").bitcast(I32))
+        tab_w.append(load_words(AT_TAB1, tab_words[1], "tab_w1"))
+        nc.sync.dma_start(gain_t[:], gain.rearrange("(b p t) -> p b t", b=2, t=4))
         nc.sync.dma_start(list3[:], offs3)
 
         def quantise(grouped, name):
-            codes = keep.tile([P, N], U32, name=name + "_codes", align_bytes=64)
-            scales = keep.tile([P, N], U8, name=name + "_scales", align_bytes=64)
+            codes = kept([P, N], U32, name + "_codes")
+            scales = kept([P, N], U8, name + "_scales")
             nc.vector.quantize_mx(out=codes[:].bitcast(FP8X4), scales=scales[:], in_=grouped[:])
             return codes, scales
 
-        def bf16_tile(name):
-            return work.tile([P, 4 * N], BF16, name=name, tag="bf", bufs=4, align_bytes=64)
-
-        def quantise_weight(raw, name, room=None):
-            grouped = bf16_tile("grouped") if room is None else in_room(room, [P, 4 * N], BF16, "grouped_" + name)
+        def quantise_weight(raw, grouped, name):
             nc.scalar.copy(
                 grouped[:].rearrange("p (t m j) -> p m j t", t=4, j=4),
                 raw[:].rearrange("p j (m t) -> p m j t", t=4),
             )
             return quantise(grouped, name)
 
-        picked_sc = keep.tile([P, S], U8, name="picked_sc", align_bytes=64)
-        nc.vector.tensor_copy(picked_sc[:], tab_sc[:].indirect(list1[:]))
+        picked_sc = kept([P, 2 * S], U8, "picked_sc")
         for a in range(2):
-            for r in range(4):
-                nc.sync.dma_start(v_sc[a][r:P:32, :].bitcast(I32), picked_sc[8 * r + a : P : 32, :].bitcast(I32))
-        v2_w = keep.tile([P, S], U32, name="v2_w", align_bytes=64)
-        nc.vector.tensor_copy(v2_w[:], tab2_w[:].bitcast(U32).indirect(list2[:]))
-        v2_sc = keep.tile([P, S], U8, name="v2_sc", align_bytes=64)
-        nc.vector.tensor_copy(v2_sc[:], tab2_sc[:].indirect(list2[:]))
-        w2_q = [quantise_weight(w2_raw, "w2_0")]
-        w2_raw = load_weight(8, w2, 0, 1, "w2_raw1")
-        w3_raw = {(a, 0): load_weight(3 + a, w3, a, 0, "w3_raw%d0" % a) for a in range(2)}
+            nc.vector.tensor_copy(picked_sc[:, S * a : S * (a + 1)], tab_sc[a][:].indirect(list1[:]))
+        for d in range(4):
+            nc.sync.dma_start(
+                v_sc[32 * d : 32 * d + 4, :].bitcast(I32), picked_sc[32 * d : 32 * (d + 1) : 8, :].bitcast(I32)
+            )
+        w2_raw.append(load_weight(AT_W2_SECOND, w2, 0, 1, "w2_raw1"))
+        w3_raw = {(1, 0): load_weight(AT_W3_NEXT, w3, 1, 0, "w3_raw10")}
 
-        v_w = keep.tile([P, 2 * S], U32, name="v_w", align_bytes=64)
+        def entries(offsets, half):
+            return offsets[:, half * N // 16 : (half + 1) * N // 16]
 
-        def gather_words(a, half):
-            first = S * a + N * half
-            cols = slice(half * N // 16, (half + 1) * N // 16)
-            nc.vector.tensor_copy(v_w[:, first : first + N], tab_w[a][:].bitcast(U32).indirect(list1[:, cols]))
+        def gather_bell(half):
+            nc.vector.tensor_copy(v2_w[half][:], tab2_w[:].bitcast(U32).indirect(entries(list2, half)))
+            nc.vector.tensor_copy(v2_sc[half][:], tab2_sc[:].indirect(entries(list2, half)))
 
-        w1_w = in_room(10, [P, 2 * 2 * H], U8, "w1_w")
-        w1_sc = keep.tile([P, 2 * H], U8, name="w1_sc", align_bytes=64)
+        def gather_stroke(a, half):
+            window = tab_w[a][:].bitcast(U32)
+            nc.vector.tensor_copy(v_w[half][:, N * a : N * (a + 1)], window.indirect(entries(list1, half)))
+
+        v2_w = [kept([P, N], U32, "v2_w0")]
+        v2_sc = [kept([P, N], U8, "v2_sc0")]
+        v_w = [kept([P, 2 * N], U32, "v_w0")]
+        gather_bell(0)
+        w2_q = [quantise_weight(w2_raw[0], bf16_tile("grouped"), "w2_0")]
+        w3_raw[0, 0] = load_weight(AT_W2_FIRST, w3, 0, 0, "w3_raw00")
+        for a in range(2):
+            gather_stroke(a, 0)
+
+        w1_w = kept([P, 2 * 2 * H], U8, "w1_w")
+        w1_sc = kept([P, 2 * H], U8, "w1_sc")
         nc.vector.tensor_copy(
             w1_w[:].bitcast(U16).rearrange("p (g t m) -> p g t m", g=4, t=4),
             w1_raw[:].rearrange("p a c -> p (a c)").bitcast(U16).rearrange("p (g m t) -> p g t m", g=4, t=4),
         )
-        gather_words(0, 0)
-        gather_words(1, 0)
         nc.vector.tensor_copy(
             w1_sc[:].rearrange("p (g t m) -> p g t m", g=4, t=4),
             w1_sc_raw[:].rearrange("p (g m t) -> p g t m", g=4, t=4),
         )
-        w2_q.append(quantise_weight(w2_raw, "w2_1"))
-        gather_words(0, 1)
-        gather_words(1, 1)
-        wgo_t = [load_wgo(0, 0)]
-        load_page(2, 0)
-        w3_raw[0, 1] = load_weight(7, w3, 0, 1, "w3_raw01")
-        w3_raw[1, 1] = load_weight(8, w3, 1, 1, "w3_raw11")
-        load_page(1, 1)
+        w2_q.append(quantise_weight(w2_raw[1], bf16_tile("grouped"), "w2_1"))
+        load_page(AT_W1, 0)
 
-        def bank(tag, bufs):
-            return psum.tile([P, N], F32, name=tag, tag=tag, bufs=bufs)
+        v_w.append(placed(AT_SECOND_PICKS, [P, 2 * N], U32, "v_w1"))
+        v2_sc.append(placed(AT_SECOND_PICKS + 4, [P, N], U8, "v2_sc1"))
+        v2_w.append(placed(AT_SECOND_PICKS + 4.5, [P, N], U32, "v2_w1"))
+        gather_stroke(0, 1)
+        wgo_t = [load_wgo(AT_TAB0, 0)]
+        gather_stroke(1, 1)
+        load_page(AT_TAB1, 1)
+        gather_bell(1)
+        w3_raw[0, 1] = load_weight(AT_TAB2, w3, 0, 1, "w3_raw01")
+        w3_raw[1, 1] = load_weight(AT_W2_SECOND, w3, 1, 1, "w3_raw11")
 
-        def bell_pass(acc, m, half, start, stop):
+        def bell_pass(acc, m, half, stop):
             codes, scales = w2_q[m // 4]
             cols = slice(P * (m % 4), P * (m % 4 + 1))
-            picks = slice(N * half, N * (half + 1))
             nc.tensor.matmul_mx(
                 out=acc[:], lhsT=codes[:, cols].bitcast(FP8X4), lhsT_scale=scales[:, cols],
-                rhs=v2_w[:, picks].bitcast(FP8X4), rhs_scale=v2_sc[:, picks], start=start, stop=stop,
+                rhs=v2_w[half][:].bitcast(FP8X4), rhs_scale=v2_sc[half][:], start=True, stop=stop,
             )
 
         def stroke_passes(acc, m, half, start):
@@ -180,45 +217,40 @@ def tile_list_carillon_strike_coach_kernel(
                 nc.tensor.matmul_mx(
                     out=acc[:], lhsT=w1_w[:, 2 * first : 2 * (first + P)].bitcast(FP4X4),
                     lhsT_scale=w1_sc[:, first : first + P],
-                    rhs=v_w[:, picks : picks + N].bitcast(FP8X4), rhs_scale=v_sc[a][:, N * half : N * (half + 1)],
+                    rhs=v_w[half][:, N * a : N * (a + 1)].bitcast(FP8X4), rhs_scale=v_sc[:, picks : picks + N],
                     start=(start and a == 0), stop=(a == 1),
                 )
-
-        def f32_tile(tag, bufs, dtype=F32):
-            return work.tile([P, N], dtype, name=tag, tag=tag, bufs=bufs)
 
         def column(vector, m):
             return vector[:, m // 4, m % 4 : m % 4 + 1]
 
-        angle, rest, factor = {}, {}, {}
-
-        def take_angle(m, half):
-            bell = bank("bell", 2)
-            bell_pass(bell, m, half, True, True)
-            angle[m, half] = f32_tile("angle", 16)
-            nc.scalar.activation(angle[m, half][:], bell[:], ACT.Identity, bias=column(phase_t, m))
+        angle, rest, cosine = {}, {}, {}
 
         def reduce_angle(m, half):
-            turns = f32_tile("turns", 3, I32)
-            nc.gpsimd.tensor_scalar(turns[:], angle[m, half][:], 1.0 / TWO_PI, 0.25, ALU.mult, ALU.add)
-            rest[m, half] = f32_tile("rest", 3)
-            nc.vector.scalar_tensor_tensor(rest[m, half][:], turns[:], -TWO_PI, angle[m, half][:], ALU.mult, ALU.add)
+            size = half_tile("size", 3)
+            if half == 0:
+                bell = bank("bell", 2)
+                bell_pass(bell, m, half, True)
+                nc.scalar.activation(size[:], bell[:], ACT.Abs, bias=column(phase_t, m))
+            else:
+                nc.scalar.activation(size[:], angle[m][:], ACT.Abs)
+            turns = half_tile("turns", 3, I32)
+            nc.scalar.activation(turns[:].bitcast(U32), size[:], ACT.Copy, bias=0.25, scale=1.0 / TWO_PI)
+            rest[m, half] = half_tile("rest", EARLY_ANGLES)
+            nc.vector.scalar_tensor_tensor(rest[m, half][:], turns[:], -TWO_PI, size[:], ALU.mult, ALU.add)
 
         def take_cosine(m, half):
-            cosine = f32_tile("cosine", 2)
-            nc.scalar.activation(cosine[:], rest[m, half][:], ACT.Sin, bias=math.pi / 2)
-            factor[m, half] = f32_tile("factor", 4)
-            nc.gpsimd.tensor_tensor(factor[m, half][:], cosine[:], wgo_t[half][:, N * (m % 4) : N * (m % 4 + 1)], ALU.mult)
+            cosine[m, half] = half_tile("cosine", 3)
+            nc.scalar.activation(cosine[m, half][:], rest[m, half][:], ACT.Sin, bias=math.pi / 2)
 
-        w3_q, h_q = {}, {}
+        w3_q, h_q, planes = {}, {}, {}
 
         def first_features(b):
-            bent = in_room(5 + b, [P, 4, N], F32, "bent4_%d" % b)
+            bent = placed(AT_BENT[b], [P, 4, N], F32, "bent%d" % b)
             for t in range(4):
-                m = 4 * b + t
                 acc = bank("sum", 3)
-                bell_pass(acc, m, 0, True, False)
-                stroke_passes(acc, m, 0, False)
+                bell_pass(acc, 4 * b + t, 0, False)
+                stroke_passes(acc, 4 * b + t, 0, False)
                 nc.scalar.activation(bent[:, t, :], acc[:], ACT.Tanh)
             grouped = bf16_tile("grouped")
             nc.vector.tensor_tensor(
@@ -228,22 +260,23 @@ def tile_list_carillon_strike_coach_kernel(
                 ALU.mult,
             )
             h_q[b, 0] = quantise(grouped, "h%d0" % b)
-            load_page(5 + b, 4 + b)
-
-        planes = {}
+            load_page(AT_BENT[b], 4 + b)
 
         def second_features(m):
             b, t = divmod(m, 4)
             if t == 0:
                 planes[b] = bf16_tile("planes")
-            take_angle(m, 1)
+            bell = bank("sum", 3)
+            bell_pass(bell, m, 1, True)
+            angle[m] = half_tile("angle", TILES)
+            nc.scalar.activation(angle[m][:], bell[:], ACT.Identity, bias=column(phase_t, m))
             acc = bank("sum", 3)
             stroke_passes(acc, m, 1, True)
-            joint = f32_tile("joint", 3)
-            nc.vector.scalar_tensor_tensor(joint[:], acc[:], column(phase_t, m), angle[m, 1][:], ALU.subtract, ALU.add)
-            bent = f32_tile("bent", 2)
-            nc.scalar.activation(bent[:], joint[:], ACT.Tanh)
-            nc.scalar.activation(planes[b][:, N * t : N * (t + 1)], bent[:], ACT.Copy, scale=column(gain_t, m))
+            joint = half_tile("joint", 3)
+            nc.vector.scalar_tensor_tensor(joint[:], acc[:], column(phase_t, m), angle[m][:], ALU.subtract, ALU.add)
+            tanh = half_tile("tanh", 2)
+            nc.scalar.activation(tanh[:], joint[:], ACT.Tanh)
+            nc.scalar.activation(planes[b][:, N * t : N * (t + 1)], tanh[:], ACT.Copy, scale=column(gain_t, m))
             if t == 3:
                 grouped = bf16_tile("grouped")
                 nc.scalar.copy(
@@ -262,37 +295,34 @@ def tile_list_carillon_strike_coach_kernel(
                     rhs=h_q[a, half][0][:].bitcast(FP8X4), rhs_scale=h_q[a, half][1][:],
                     start=(a == 0), stop=(a == 1),
                 )
-            window = pages[m][:].indirect(list3[:, half * N // 16 : (half + 1) * N // 16])
-            z = f32_tile("z", 3)
-            y = f32_tile("y_sb", 2)
-            nc.scalar.copy(y[:], acc[:])
-            nc.gpsimd.tensor_tensor(z[:], y[:], factor[m, half][:], ALU.mult)
-            nc.vector.tensor_copy(window, z[:])
+            z = half_tile("z", 2)
+            nc.vector.tensor_tensor(z[:], acc[:], cosine[m, half][:], ALU.mult)
+            window = pages[m][:].indirect(entries(list3, half))
+            nc.vector.tensor_tensor(window, z[:], wgo_t[half][:, N * t : N * (t + 1)], ALU.mult)
             if half == 1:
                 nc.sync.dma_start(out_rows[b, t], pages[m][:])
 
         for b in range(2):
             first_features(b)
-        for a in range(2):
-            w3_q[a, 0] = quantise_weight(w3_raw[a, 0], "w3_%d0" % a)
-            load_page(3 + a, 2 + a)
-        for m in range(8):
-            take_angle(m, 0)
-        for u in range(3):
-            reduce_angle(u, 0)
-        for u in range(2):
-            take_cosine(u, 0)
-        for u in range(16):
-            if u + 3 < 16:
-                reduce_angle((u + 3) % 8, (u + 3) // 8)
-            if u + 2 < 16:
-                take_cosine((u + 2) % 8, (u + 2) // 8)
-            place(u % 8, u // 8)
-            if u in (0, 1):
-                a = (0, 1).index(u)
-                w3_q[a, 1] = quantise_weight(w3_raw[a, 1], "w3_%d1" % a, 9 if a == 1 else None)
-                load_page(7 + a, 6 + a)
-                if a == 1:
-                    wgo_t.append(load_wgo(9, 1))
-            for j in {0: (0,), 1: (1,), 2: (2, 3), 3: (4,), 4: (5, 6), 5: (7,)}.get(u, ()):
-                second_features(j)
+        for a, start in enumerate((AT_W2_FIRST, AT_W3_NEXT)):
+            w3_q[a, 0] = quantise_weight(w3_raw[a, 0], bf16_tile("grouped"), "w3_%d0" % a)
+            load_page(start, 2 + a)
+        for m in range(EARLY_ANGLES):
+            reduce_angle(m, 0)
+        take_cosine(0, 0)
+
+        for u in range(2 * TILES):
+            if EARLY_ANGLES <= u + ANGLE_LEAD < 2 * TILES:
+                reduce_angle((u + ANGLE_LEAD) % TILES, (u + ANGLE_LEAD) // TILES)
+            if u + 1 < 2 * TILES:
+                take_cosine((u + 1) % TILES, (u + 1) // TILES)
+            place(u % TILES, u // TILES)
+            if u == 0:
+                w3_q[0, 1] = quantise_weight(w3_raw[0, 1], bf16_tile("grouped"), "w3_01")
+                load_page(AT_TAB2, 6)
+            if u == 1:
+                w3_q[1, 1] = quantise_weight(w3_raw[1, 1], placed(AT_W3_LAST, [P, 4 * N], BF16, "w3_last"), "w3_11")
+                load_page(AT_W2_SECOND, 7)
+                wgo_t.append(load_wgo(AT_W3_LAST, 1))
+            for m in SECOND_FEATURES_AFTER.get(u, ()):
+                second_features(m)

@@ -36,9 +36,9 @@ AT_TAB_SCALES1 = 71
 AT_SECOND_PICKS = 80
 AT_W1_SCALES = 83.5
 
-SECOND_FEATURES_AFTER = {0: (0,), 1: (1,), 2: (2, 3), 3: (4,), 4: (5, 6), 5: (7,)}
+FEATURES_PER_STEP = 2
 EARLY_ANGLES = 4
-ANGLE_LEAD = 2
+ANGLE_LEAD = 3
 
 
 def tile_list_carillon_strike_coach_kernel(
@@ -114,26 +114,26 @@ def tile_list_carillon_strike_coach_kernel(
 
         nc.sync.dma_start(list1[:], offs)
         nc.sync.dma_start(list2[:], offs2)
+        nc.sync.dma_start(list3[:], offs3)
+        nc.sync.dma_start(phase_t[:], phase.rearrange("(b p t) -> p b t", b=2, t=4))
+        nc.sync.dma_start(gain_t[:], gain.rearrange("(b p t) -> p b t", b=2, t=4))
         for a in range(2):
             nc.sync.dma_start(tab_sc[a][0:P:8, :].bitcast(I32), tab_scales[a].bitcast(I32))
-        w2_raw = [load_weight(AT_W2_FIRST, w2, 0, 0, "w2_raw0")]
+        tab2_w = load_words(AT_TAB2, tab2_words[0], "tab2_w")
         for d in range(4):
             nc.sync.dma_start(
                 tab2_sc[32 * d : 32 * d + 4, :].bitcast(I32), tab2_scales[0, 4 * d : 4 * d + 4, :].bitcast(I32)
             )
-        tab2_w = load_words(AT_TAB2, tab2_words[0], "tab2_w")
-        nc.sync.dma_start(phase_t[:], phase.rearrange("(b p t) -> p b t", b=2, t=4))
+        w2_raw = [load_weight(AT_W2_FIRST, w2, 0, 0, "w2_raw0")]
         tab_w = [load_words(AT_TAB0, tab_words[0], "tab_w0")]
+        w1_raw = placed(AT_W1, [P, 2, 2 * H // 4], I32, "w1_raw")
+        nc.sync.dma_start(w1_raw[:], w1_words.rearrange("a p c -> p a c").bitcast(I32))
         for d in range(4):
             nc.sync.dma_start(
                 w1_sc_raw[32 * d : 32 * d + 4, :].bitcast(I32).rearrange("p (a c) -> p a c", a=2),
                 w1_scales[:, 4 * d : 4 * d + 4, :].rearrange("a q c -> q a c").bitcast(I32),
             )
-        w1_raw = placed(AT_W1, [P, 2, 2 * H // 4], I32, "w1_raw")
-        nc.sync.dma_start(w1_raw[:], w1_words.rearrange("a p c -> p a c").bitcast(I32))
         tab_w.append(load_words(AT_TAB1, tab_words[1], "tab_w1"))
-        nc.sync.dma_start(gain_t[:], gain.rearrange("(b p t) -> p b t", b=2, t=4))
-        nc.sync.dma_start(list3[:], offs3)
 
         def quantise(grouped, name):
             codes = kept([P, N], U32, name + "_codes")
@@ -141,10 +141,11 @@ def tile_list_carillon_strike_coach_kernel(
             nc.vector.quantize_mx(out=codes[:].bitcast(FP8X4), scales=scales[:], in_=grouped[:])
             return codes, scales
 
-        def quantise_weight(raw, grouped, name):
-            nc.scalar.copy(
-                grouped[:].rearrange("p (t m j) -> p m j t", t=4, j=4),
-                raw[:].rearrange("p j (m t) -> p m j t", t=4),
+        def quantise_weight(raw, grouped, name, on_vector=False):
+            copy, walk = (nc.vector.tensor_copy, "p m t j") if on_vector else (nc.scalar.copy, "p m j t")
+            copy(
+                grouped[:].rearrange("p (t m j) -> " + walk, t=4, j=4),
+                raw[:].rearrange("p j (m t) -> " + walk, t=4),
             )
             return quantise(grouped, name)
 
@@ -305,7 +306,7 @@ def tile_list_carillon_strike_coach_kernel(
         for b in range(2):
             first_features(b)
         for a, start in enumerate((AT_W2_FIRST, AT_W3_NEXT)):
-            w3_q[a, 0] = quantise_weight(w3_raw[a, 0], bf16_tile("grouped"), "w3_%d0" % a)
+            w3_q[a, 0] = quantise_weight(w3_raw[a, 0], bf16_tile("grouped"), "w3_%d0" % a, on_vector=(a == 0))
             load_page(start, 2 + a)
         for m in range(EARLY_ANGLES):
             reduce_angle(m, 0)
@@ -324,5 +325,5 @@ def tile_list_carillon_strike_coach_kernel(
                 w3_q[1, 1] = quantise_weight(w3_raw[1, 1], placed(AT_W3_LAST, [P, 4 * N], BF16, "w3_last"), "w3_11")
                 load_page(AT_W2_SECOND, 7)
                 wgo_t.append(load_wgo(AT_W3_LAST, 1))
-            for m in SECOND_FEATURES_AFTER.get(u, ()):
+            for m in range(FEATURES_PER_STEP * u, min(FEATURES_PER_STEP * (u + 1), TILES)):
                 second_features(m)

@@ -36,9 +36,8 @@ AT_TAB_SCALES1 = 71
 AT_SECOND_PICKS = 80
 AT_W1_SCALES = 83.5
 
-FEATURES_PER_STEP = 2
-EARLY_ANGLES = 4
-ANGLE_LEAD = 3
+FEATURE_STEPS = 4
+ANGLE_LEAD = 2
 
 
 def tile_list_carillon_strike_coach_kernel(
@@ -64,8 +63,8 @@ def tile_list_carillon_strike_coach_kernel(
         def half_tile(tag, bufs, dtype=F32):
             return work.tile([P, N], dtype, name=tag, tag=tag, bufs=bufs)
 
-        def bank(tag, bufs):
-            return psum.tile([P, N], F32, name=tag, tag=tag, bufs=bufs)
+        def bank(tag):
+            return psum.tile([P, N], F32, name=tag, tag=tag, bufs={"sum": 5, "y": 3}[tag])
 
         list1 = keep.tile([P, S // 16], U16, name="list1")
         list2 = keep.tile([P, S // 16], U16, name="list2")
@@ -113,27 +112,16 @@ def tile_list_carillon_strike_coach_kernel(
             nc.sync.dma_start(pages[m][:], page_rows[m // 4, m % 4])
 
         nc.sync.dma_start(list1[:], offs)
-        nc.sync.dma_start(list2[:], offs2)
-        nc.sync.dma_start(list3[:], offs3)
-        nc.sync.dma_start(phase_t[:], phase.rearrange("(b p t) -> p b t", b=2, t=4))
-        nc.sync.dma_start(gain_t[:], gain.rearrange("(b p t) -> p b t", b=2, t=4))
         for a in range(2):
             nc.sync.dma_start(tab_sc[a][0:P:8, :].bitcast(I32), tab_scales[a].bitcast(I32))
+        nc.sync.dma_start(list2[:], offs2)
+        w2_raw = [load_weight(AT_W2_FIRST, w2, 0, 0, "w2_raw0")]
         tab2_w = load_words(AT_TAB2, tab2_words[0], "tab2_w")
         for d in range(4):
             nc.sync.dma_start(
                 tab2_sc[32 * d : 32 * d + 4, :].bitcast(I32), tab2_scales[0, 4 * d : 4 * d + 4, :].bitcast(I32)
             )
-        w2_raw = [load_weight(AT_W2_FIRST, w2, 0, 0, "w2_raw0")]
-        tab_w = [load_words(AT_TAB0, tab_words[0], "tab_w0")]
-        w1_raw = placed(AT_W1, [P, 2, 2 * H // 4], I32, "w1_raw")
-        nc.sync.dma_start(w1_raw[:], w1_words.rearrange("a p c -> p a c").bitcast(I32))
-        for d in range(4):
-            nc.sync.dma_start(
-                w1_sc_raw[32 * d : 32 * d + 4, :].bitcast(I32).rearrange("p (a c) -> p a c", a=2),
-                w1_scales[:, 4 * d : 4 * d + 4, :].rearrange("a q c -> q a c").bitcast(I32),
-            )
-        tab_w.append(load_words(AT_TAB1, tab_words[1], "tab_w1"))
+        tab_w = [load_words(start, tab_words[a], "tab_w%d" % a) for a, start in enumerate((AT_TAB0, AT_TAB1))]
 
         def quantise(grouped, name):
             codes = kept([P, N], U32, name + "_codes")
@@ -156,8 +144,19 @@ def tile_list_carillon_strike_coach_kernel(
             nc.sync.dma_start(
                 v_sc[32 * d : 32 * d + 4, :].bitcast(I32), picked_sc[32 * d : 32 * (d + 1) : 8, :].bitcast(I32)
             )
+
+        nc.sync.dma_start(phase_t[:], phase.rearrange("(b p t) -> p b t", b=2, t=4))
+        w1_raw = placed(AT_W1, [P, 2, 2 * H // 4], I32, "w1_raw")
+        nc.sync.dma_start(w1_raw[:], w1_words.rearrange("a p c -> p a c").bitcast(I32))
+        for d in range(4):
+            nc.sync.dma_start(
+                w1_sc_raw[32 * d : 32 * d + 4, :].bitcast(I32).rearrange("p (a c) -> p a c", a=2),
+                w1_scales[:, 4 * d : 4 * d + 4, :].rearrange("a q c -> q a c").bitcast(I32),
+            )
         w2_raw.append(load_weight(AT_W2_SECOND, w2, 0, 1, "w2_raw1"))
         w3_raw = {(1, 0): load_weight(AT_W3_NEXT, w3, 1, 0, "w3_raw10")}
+        nc.sync.dma_start(gain_t[:], gain.rearrange("(b p t) -> p b t", b=2, t=4))
+        nc.sync.dma_start(list3[:], offs3)
 
         def entries(offsets, half):
             return offsets[:, half * N // 16 : (half + 1) * N // 16]
@@ -230,26 +229,26 @@ def tile_list_carillon_strike_coach_kernel(
         def reduce_angle(m, half):
             size = half_tile("size", 3)
             if half == 0:
-                bell = bank("bell", 2)
+                bell = bank("sum")
                 bell_pass(bell, m, half, True)
                 nc.scalar.activation(size[:], bell[:], ACT.Abs, bias=column(phase_t, m))
             else:
                 nc.scalar.activation(size[:], angle[m][:], ACT.Abs)
             turns = half_tile("turns", 3, I32)
             nc.scalar.activation(turns[:].bitcast(U32), size[:], ACT.Copy, bias=0.25, scale=1.0 / TWO_PI)
-            rest[m, half] = half_tile("rest", EARLY_ANGLES)
+            rest[m, half] = half_tile("rest", ANGLE_LEAD + 1)
             nc.vector.scalar_tensor_tensor(rest[m, half][:], turns[:], -TWO_PI, size[:], ALU.mult, ALU.add)
 
         def take_cosine(m, half):
             cosine[m, half] = half_tile("cosine", 3)
             nc.scalar.activation(cosine[m, half][:], rest[m, half][:], ACT.Sin, bias=math.pi / 2)
 
-        w3_q, h_q, planes = {}, {}, {}
+        w3_q, h_q, planes, joint = {}, {}, {}, {}
 
         def first_features(b):
             bent = placed(AT_BENT[b], [P, 4, N], F32, "bent%d" % b)
             for t in range(4):
-                acc = bank("sum", 3)
+                acc = bank("sum")
                 bell_pass(acc, 4 * b + t, 0, False)
                 stroke_passes(acc, 4 * b + t, 0, False)
                 nc.scalar.activation(bent[:, t, :], acc[:], ACT.Tanh)
@@ -263,20 +262,22 @@ def tile_list_carillon_strike_coach_kernel(
             h_q[b, 0] = quantise(grouped, "h%d0" % b)
             load_page(AT_BENT[b], 4 + b)
 
+        def second_sum(m):
+            bell = bank("sum")
+            bell_pass(bell, m, 1, True)
+            angle[m] = half_tile("angle", TILES)
+            nc.scalar.activation(angle[m][:], bell[:], ACT.Identity, bias=column(phase_t, m))
+            acc = bank("sum")
+            stroke_passes(acc, m, 1, True)
+            joint[m] = half_tile("joint", 4)
+            nc.vector.scalar_tensor_tensor(joint[m][:], acc[:], column(phase_t, m), angle[m][:], ALU.subtract, ALU.add)
+
         def second_features(m):
             b, t = divmod(m, 4)
             if t == 0:
                 planes[b] = bf16_tile("planes")
-            bell = bank("sum", 3)
-            bell_pass(bell, m, 1, True)
-            angle[m] = half_tile("angle", TILES)
-            nc.scalar.activation(angle[m][:], bell[:], ACT.Identity, bias=column(phase_t, m))
-            acc = bank("sum", 3)
-            stroke_passes(acc, m, 1, True)
-            joint = half_tile("joint", 3)
-            nc.vector.scalar_tensor_tensor(joint[:], acc[:], column(phase_t, m), angle[m][:], ALU.subtract, ALU.add)
             tanh = half_tile("tanh", 2)
-            nc.scalar.activation(tanh[:], joint[:], ACT.Tanh)
+            nc.scalar.activation(tanh[:], joint[m][:], ACT.Tanh)
             nc.scalar.activation(planes[b][:, N * t : N * (t + 1)], tanh[:], ACT.Copy, scale=column(gain_t, m))
             if t == 3:
                 grouped = bf16_tile("grouped")
@@ -288,7 +289,7 @@ def tile_list_carillon_strike_coach_kernel(
 
         def place(m, half):
             b, t = divmod(m, 4)
-            acc = bank("y", 3)
+            acc = bank("y")
             cols = slice(P * t, P * (t + 1))
             for a in range(2):
                 nc.tensor.matmul_mx(
@@ -303,20 +304,26 @@ def tile_list_carillon_strike_coach_kernel(
             if half == 1:
                 nc.sync.dma_start(out_rows[b, t], pages[m][:])
 
+        reduce_angle(0, 0)
         for b in range(2):
             first_features(b)
+        reduce_angle(1, 0)
         for a, start in enumerate((AT_W2_FIRST, AT_W3_NEXT)):
             w3_q[a, 0] = quantise_weight(w3_raw[a, 0], bf16_tile("grouped"), "w3_%d0" % a, on_vector=(a == 0))
             load_page(start, 2 + a)
-        for m in range(EARLY_ANGLES):
-            reduce_angle(m, 0)
         take_cosine(0, 0)
 
+        def feature_tiles(step):
+            return range(step * TILES // FEATURE_STEPS, (step + 1) * TILES // FEATURE_STEPS)
+
         for u in range(2 * TILES):
-            if EARLY_ANGLES <= u + ANGLE_LEAD < 2 * TILES:
+            if u + ANGLE_LEAD < 2 * TILES:
                 reduce_angle((u + ANGLE_LEAD) % TILES, (u + ANGLE_LEAD) // TILES)
             if u + 1 < 2 * TILES:
                 take_cosine((u + 1) % TILES, (u + 1) // TILES)
+            if u < FEATURE_STEPS:
+                for m in feature_tiles(u):
+                    second_sum(m)
             place(u % TILES, u // TILES)
             if u == 0:
                 w3_q[0, 1] = quantise_weight(w3_raw[0, 1], bf16_tile("grouped"), "w3_01")
@@ -325,5 +332,6 @@ def tile_list_carillon_strike_coach_kernel(
                 w3_q[1, 1] = quantise_weight(w3_raw[1, 1], placed(AT_W3_LAST, [P, 4 * N], BF16, "w3_last"), "w3_11")
                 load_page(AT_W2_SECOND, 7)
                 wgo_t.append(load_wgo(AT_W3_LAST, 1))
-            for m in range(FEATURES_PER_STEP * u, min(FEATURES_PER_STEP * (u + 1), TILES)):
-                second_features(m)
+            if 1 <= u <= FEATURE_STEPS:
+                for m in feature_tiles(u - 1):
+                    second_features(m)

import math
from contextlib import ExitStack

import concourse.mybir as mybir

K, K2, H, T, S, T2 = 1024, 512, 1024, 2048, 1024, 2048
FLOPS = 2 * S * H * (K + K2 + H)

F32 = mybir.dt.float32
BF16 = mybir.dt.bfloat16
I32 = mybir.dt.int32
U32 = mybir.dt.uint32
U16 = mybir.dt.uint16
U8 = mybir.dt.uint8
FP8X4 = mybir.dt.float8_e4m3fn_x4
FP4X4 = mybir.dt.float4_e2m1fn_x4
ALU = mybir.AluOpType
ACT = mybir.ActivationFunctionType

P = 128
N = 512
TILES = H // P
TWO_PI = 2.0 * math.pi
KIB = 1024

AT_TAB0 = 0
AT_TAB1 = 8
AT_W1 = 16
AT_TAB2 = 24
AT_W2_FIRST = 32
AT_BENT = (40, 48)
AT_W3_LAST = 56
AT_W2_SECOND = 64
AT_W3_NEXT = 72
AT_TAB_SCALES1 = 71
AT_SECOND_PICKS = 80
AT_W1_SCALES = 83.5

FEATURE_STEPS = 4
ANGLE_LEAD = 2


def tile_list_carillon_strike_coach_kernel(
    tc, tab_words, tab_scales, tab2_words, tab2_scales, offs, offs2, offs3,
    w1_words, w1_scales, w2, gain, w3, phase, page1, wgo, out,
):
    nc = tc.nc
    with ExitStack() as ctx:
        keep = ctx.enter_context(tc.tile_pool(name="keep", bufs=1))
        shared = ctx.enter_context(tc.tile_pool(name="shared", bufs=1))
        work = ctx.enter_context(tc.tile_pool(name="work", bufs=2))
        psum = ctx.enter_context(tc.psum_pool(name="psum", bufs=1))

        def placed(start, shape, dtype, name):
            return shared.tile(shape, dtype, name=name, offset=int(start * KIB), align_bytes=64)

        def kept(shape, dtype, name):
            return keep.tile(shape, dtype, name=name, align_bytes=64)

        def bf16_tile(name):
            return work.tile([P, 4 * N], BF16, name=name, tag="bf16", bufs=4, align_bytes=64)

        def half_tile(tag, bufs, dtype=F32):
            return work.tile([P, N], dtype, name=tag, tag=tag, bufs=bufs)

        def bank(tag):
            return psum.tile([P, N], F32, name=tag, tag=tag, bufs={"sum": 5, "y": 3}[tag])

        list1 = keep.tile([P, S // 16], U16, name="list1")
        list2 = keep.tile([P, S // 16], U16, name="list2")
        list3 = keep.tile([P, S // 16], U16, name="list3")
        gain_t = keep.tile([P, 2, 4], F32, name="gain_t")
        phase_t = keep.tile([P, 2, 4], F32, name="phase_t")

        tab_sc = [kept([P, T], U8, "tab_sc0"), placed(AT_TAB_SCALES1, [P, T], U8, "tab_sc1")]
        tab2_sc = kept([P, T], U8, "tab2_sc")
        w1_sc_raw = placed(AT_W1_SCALES, [P, 2 * H], U8, "w1_sc_raw")
        v_sc = kept([P, 2 * S], U8, "v_sc")
        nc.gpsimd.memset(tab_sc[0][:].bitcast(I32), 0)
        nc.gpsimd.memset(tab2_sc[:].bitcast(I32), 0)
        for tile in (tab_sc[1], w1_sc_raw, v_sc):
            nc.vector.memset(tile[:].bitcast(I32), 0)

        warm = keep.tile([P, 2], F32, name="warm")
        nc.vector.memset(warm[:, 0:1], 0.0)
        nc.scalar.activation(warm[:, 1:2], warm[:, 0:1], ACT.Silu)

        def load_words(start, words, name):
            tile = placed(start, [P, T], I32, name)
            nc.sync.dma_start(tile[:], words.rearrange("p t i -> p (t i)").bitcast(I32))
            return tile

        def load_weight(start, w, a, b, name):
            tile = placed(start, [P, 4, N], F32, name)
            rows = w[N * a : N * (a + 1), N * b : N * (b + 1)]
            nc.sync.dma_start(tile[:], rows.rearrange("(p j) c -> p j c", j=4))
            return tile

        def load_wgo(start, half):
            tile = placed(start, [P, 4 * N], F32, "wgo%d" % half)
            rows = wgo[:, N * half : N * (half + 1)].rearrange("(p t) j -> p t j", t=4)
            for d in range(4):
                nc.sync.dma_start(tile[32 * d : 32 * (d + 1), :].rearrange("p (t j) -> p t j", t=4), rows)
            return tile

        page_rows = page1.rearrange("(b p t) c -> b t p c", b=2, t=4)
        out_rows = out.rearrange("(b p t) c -> b t p c", b=2, t=4)
        pages = {}

        def load_page(start, m):
            pages[m] = placed(start, [P, T2], F32, "page%d" % m)
            nc.sync.dma_start(pages[m][:], page_rows[m // 4, m % 4])

        nc.sync.dma_start(list1[:], offs)
        for a in range(2):
            nc.sync.dma_start(tab_sc[a][0:P:8, :].bitcast(I32), tab_scales[a].bitcast(I32))
        nc.sync.dma_start(list2[:], offs2)
        w2_raw = [load_weight(AT_W2_FIRST, w2, 0, 0, "w2_raw0")]
        tab2_w = load_words(AT_TAB2, tab2_words[0], "tab2_w")
        for d in range(4):
            nc.sync.dma_start(
                tab2_sc[32 * d : 32 * d + 4, :].bitcast(I32), tab2_scales[0, 4 * d : 4 * d + 4, :].bitcast(I32)
            )
        tab_w = [load_words(start, tab_words[a], "tab_w%d" % a) for a, start in enumerate((AT_TAB0, AT_TAB1))]

        def quantise(grouped, name):
            codes = kept([P, N], U32, name + "_codes")
            scales = kept([P, N], U8, name + "_scales")
            nc.vector.quantize_mx(out=codes[:].bitcast(FP8X4), scales=scales[:], in_=grouped[:])
            return codes, scales

        def quantise_weight(raw, grouped, name, on_vector=False):
            copy, walk = (nc.vector.tensor_copy, "p m t j") if on_vector else (nc.scalar.copy, "p m j t")
            copy(
                grouped[:].rearrange("p (t m j) -> " + walk, t=4, j=4),
                raw[:].rearrange("p j (m t) -> " + walk, t=4),
            )
            return quantise(grouped, name)

        picked_sc = kept([P, 2 * S], U8, "picked_sc")
        for a in range(2):
            nc.vector.tensor_copy(picked_sc[:, S * a : S * (a + 1)], tab_sc[a][:].indirect(list1[:]))
        for d in range(4):
            nc.sync.dma_start(
                v_sc[32 * d : 32 * d + 4, :].bitcast(I32), picked_sc[32 * d : 32 * (d + 1) : 8, :].bitcast(I32)
            )

        nc.sync.dma_start(phase_t[:], phase.rearrange("(b p t) -> p b t", b=2, t=4))
        w1_raw = placed(AT_W1, [P, 2, 2 * H // 4], I32, "w1_raw")
        nc.sync.dma_start(w1_raw[:], w1_words.rearrange("a p c -> p a c").bitcast(I32))
        for d in range(4):
            nc.sync.dma_start(
                w1_sc_raw[32 * d : 32 * d + 4, :].bitcast(I32).rearrange("p (a c) -> p a c", a=2),
                w1_scales[:, 4 * d : 4 * d + 4, :].rearrange("a q c -> q a c").bitcast(I32),
            )
        w2_raw.append(load_weight(AT_W2_SECOND, w2, 0, 1, "w2_raw1"))
        w3_raw = {(1, 0): load_weight(AT_W3_NEXT, w3, 1, 0, "w3_raw10")}
        nc.sync.dma_start(gain_t[:], gain.rearrange("(b p t) -> p b t", b=2, t=4))
        nc.sync.dma_start(list3[:], offs3)

        def entries(offsets, half):
            return offsets[:, half * N // 16 : (half + 1) * N // 16]

        def gather_bell(half):
            nc.vector.tensor_copy(v2_w[half][:], tab2_w[:].bitcast(U32).indirect(entries(list2, half)))
            nc.vector.tensor_copy(v2_sc[half][:], tab2_sc[:].indirect(entries(list2, half)))

        def gather_stroke(a, half):
            window = tab_w[a][:].bitcast(U32)
            nc.vector.tensor_copy(v_w[half][:, N * a : N * (a + 1)], window.indirect(entries(list1, half)))

        v2_w = [kept([P, N], U32, "v2_w0")]
        v2_sc = [kept([P, N], U8, "v2_sc0")]
        v_w = [kept([P, 2 * N], U32, "v_w0")]
        gather_bell(0)
        w2_q = [quantise_weight(w2_raw[0], bf16_tile("grouped"), "w2_0")]
        w3_raw[0, 0] = load_weight(AT_W2_FIRST, w3, 0, 0, "w3_raw00")
        for a in range(2):
            gather_stroke(a, 0)

        w1_w = kept([P, 2 * 2 * H], U8, "w1_w")
        w1_sc = kept([P, 2 * H], U8, "w1_sc")
        nc.vector.tensor_copy(
            w1_w[:].bitcast(U16).rearrange("p (g t m) -> p g t m", g=4, t=4),
            w1_raw[:].rearrange("p a c -> p (a c)").bitcast(U16).rearrange("p (g m t) -> p g t m", g=4, t=4),
        )
        nc.vector.tensor_copy(
            w1_sc[:].rearrange("p (g t m) -> p g t m", g=4, t=4),
            w1_sc_raw[:].rearrange("p (g m t) -> p g t m", g=4, t=4),
        )
        w2_q.append(quantise_weight(w2_raw[1], bf16_tile("grouped"), "w2_1"))
        load_page(AT_W1, 0)

        v_w.append(placed(AT_SECOND_PICKS, [P, 2 * N], U32, "v_w1"))
        v2_sc.append(placed(AT_SECOND_PICKS + 4, [P, N], U8, "v2_sc1"))
        v2_w.append(placed(AT_SECOND_PICKS + 4.5, [P, N], U32, "v2_w1"))
        gather_stroke(0, 1)
        wgo_t = [load_wgo(AT_TAB0, 0)]
        gather_stroke(1, 1)
        load_page(AT_TAB1, 1)
        gather_bell(1)
        w3_raw[0, 1] = load_weight(AT_TAB2, w3, 0, 1, "w3_raw01")
        w3_raw[1, 1] = load_weight(AT_W2_SECOND, w3, 1, 1, "w3_raw11")

        def bell_pass(acc, m, half, stop):
            codes, scales = w2_q[m // 4]
            cols = slice(P * (m % 4), P * (m % 4 + 1))
            nc.tensor.matmul_mx(
                out=acc[:], lhsT=codes[:, cols].bitcast(FP8X4), lhsT_scale=scales[:, cols],
                rhs=v2_w[half][:].bitcast(FP8X4), rhs_scale=v2_sc[half][:], start=True, stop=stop,
            )

        def stroke_passes(acc, m, half, start):
            for a in range(2):
                first = H * a + P * m
                picks = S * a + N * half
                nc.tensor.matmul_mx(
                    out=acc[:], lhsT=w1_w[:, 2 * first : 2 * (first + P)].bitcast(FP4X4),
                    lhsT_scale=w1_sc[:, first : first + P],
                    rhs=v_w[half][:, N * a : N * (a + 1)].bitcast(FP8X4), rhs_scale=v_sc[:, picks : picks + N],
                    start=(start and a == 0), stop=(a == 1),
                )

        def column(vector, m):
            return vector[:, m // 4, m % 4 : m % 4 + 1]

        angle, rest, cosine = {}, {}, {}

        def reduce_angle(m, half):
            size = half_tile("size", 3)
            if half == 0:
                bell = bank("sum")
                bell_pass(bell, m, half, True)
                nc.scalar.activation(size[:], bell[:], ACT.Abs, bias=column(phase_t, m))
            else:
                nc.scalar.activation(size[:], angle[m][:], ACT.Abs)
            turns = half_tile("turns", 3, I32)
            nc.scalar.activation(turns[:].bitcast(U32), size[:], ACT.Copy, bias=0.25, scale=1.0 / TWO_PI)
            rest[m, half] = half_tile("rest", ANGLE_LEAD + 1)
            nc.vector.scalar_tensor_tensor(rest[m, half][:], turns[:], -TWO_PI, size[:], ALU.mult, ALU.add)

        def take_cosine(m, half):
            cosine[m, half] = half_tile("cosine", 3)
            nc.scalar.activation(cosine[m, half][:], rest[m, half][:], ACT.Sin, bias=math.pi / 2)

        w3_q, h_q, planes, joint = {}, {}, {}, {}

        def first_features(b):
            bent = placed(AT_BENT[b], [P, 4, N], F32, "bent%d" % b)
            for t in range(4):
                acc = bank("sum")
                bell_pass(acc, 4 * b + t, 0, False)
                stroke_passes(acc, 4 * b + t, 0, False)
                nc.scalar.activation(bent[:, t, :], acc[:], ACT.Tanh)
            grouped = bf16_tile("grouped")
            nc.vector.tensor_tensor(
                grouped[:].rearrange("p (c i t) -> p c t i", i=4, t=4),
                bent[:].rearrange("p t (c i) -> p c t i", i=4),
                gain_t[:, b : b + 1, :].unsqueeze(3).to_broadcast([P, N // 4, 4, 4]),
                ALU.mult,
            )
            h_q[b, 0] = quantise(grouped, "h%d0" % b)
            load_page(AT_BENT[b], 4 + b)

        def second_sum(m):
            bell = bank("sum")
            bell_pass(bell, m, 1, True)
            angle[m] = half_tile("angle", TILES)
            nc.scalar.activation(angle[m][:], bell[:], ACT.Identity, bias=column(phase_t, m))
            acc = bank("sum")
            stroke_passes(acc, m, 1, True)
            joint[m] = half_tile("joint", 4)
            nc.vector.scalar_tensor_tensor(joint[m][:], acc[:], column(phase_t, m), angle[m][:], ALU.subtract, ALU.add)

        def second_features(m):
            b, t = divmod(m, 4)
            if t == 0:
                planes[b] = bf16_tile("planes")
            tanh = half_tile("tanh", 2)
            nc.scalar.activation(tanh[:], joint[m][:], ACT.Tanh)
            nc.scalar.activation(planes[b][:, N * t : N * (t + 1)], tanh[:], ACT.Copy, scale=column(gain_t, m))
            if t == 3:
                grouped = bf16_tile("grouped")
                nc.scalar.copy(
                    grouped[:].rearrange("p (c i t) -> p c t i", i=4, t=4),
                    planes[b][:].rearrange("p (t c i) -> p c t i", i=4, t=4),
                )
                h_q[b, 1] = quantise(grouped, "h%d1" % b)

        def place(m, half):
            b, t = divmod(m, 4)
            acc = bank("y")
            cols = slice(P * t, P * (t + 1))
            for a in range(2):
                nc.tensor.matmul_mx(
                    out=acc[:], lhsT=w3_q[a, b][0][:, cols].bitcast(FP8X4), lhsT_scale=w3_q[a, b][1][:, cols],
                    rhs=h_q[a, half][0][:].bitcast(FP8X4), rhs_scale=h_q[a, half][1][:],
                    start=(a == 0), stop=(a == 1),
                )
            z = half_tile("z", 2)
            nc.vector.tensor_tensor(z[:], acc[:], cosine[m, half][:], ALU.mult)
            window = pages[m][:].indirect(entries(list3, half))
            nc.vector.tensor_tensor(window, z[:], wgo_t[half][:, N * t : N * (t + 1)], ALU.mult)
            if half == 1:
                nc.sync.dma_start(out_rows[b, t], pages[m][:])

        reduce_angle(0, 0)
        for b in range(2):
            first_features(b)
        reduce_angle(1, 0)
        for a, start in enumerate((AT_W2_FIRST, AT_W3_NEXT)):
            w3_q[a, 0] = quantise_weight(w3_raw[a, 0], bf16_tile("grouped"), "w3_%d0" % a, on_vector=(a == 0))
            load_page(start, 2 + a)
        take_cosine(0, 0)

        def feature_tiles(step):
            return range(step * TILES // FEATURE_STEPS, (step + 1) * TILES // FEATURE_STEPS)

        for u in range(2 * TILES):
            if u + ANGLE_LEAD < 2 * TILES:
                reduce_angle((u + ANGLE_LEAD) % TILES, (u + ANGLE_LEAD) // TILES)
            if u + 1 < 2 * TILES:
                take_cosine((u + 1) % TILES, (u + 1) // TILES)
            if u < FEATURE_STEPS:
                for m in feature_tiles(u):
                    second_sum(m)
            place(u % TILES, u // TILES)
            if u == 0:
                w3_q[0, 1] = quantise_weight(w3_raw[0, 1], bf16_tile("grouped"), "w3_01")
                load_page(AT_TAB2, 6)
            if u == 1:
                w3_q[1, 1] = quantise_weight(w3_raw[1, 1], placed(AT_W3_LAST, [P, 4 * N], BF16, "w3_last"), "w3_11")
                load_page(AT_W2_SECOND, 7)
                wgo_t.append(load_wgo(AT_W3_LAST, 1))
            if 1 <= u <= FEATURE_STEPS:
                for m in feature_tiles(u - 1):
                    second_features(m)
